import numpy as np
import ml_dtypes


def mxq(x, axis, fmt="e4m3"):
    dtype, down = {"e4m3": (ml_dtypes.float8_e4m3fn, 7), "e5m2": (ml_dtypes.float8_e5m2, 14)}[fmt]
    v = np.moveaxis(np.asarray(x, np.float32).astype(ml_dtypes.bfloat16).astype(np.float64), axis, -1)
    blocks = v.reshape(v.shape[:-1] + (-1, 32))
    amax = np.abs(blocks).max(-1, keepdims=True)
    byte = np.maximum(np.where(amax > 0, np.frexp(amax)[1] - 1 + 127, 0) - down, 1)
    scale = np.exp2(byte - 127.0)
    codes = (blocks / scale).astype(np.float32).astype(dtype).astype(np.float64)
    return np.moveaxis((codes * scale).reshape(v.shape), -1, axis)


WIDE = False


def mx_kscale(k):
    if not WIDE:
        return np.ones(k)
    levels = np.array([10, -10, 5, -5, 0])
    if k % 512:
        return np.exp2(np.random.permutation(np.resize(levels, k // 32))).repeat(32)
    a = np.empty((k // 512, 16))
    for p in range(k // 512):
        a[p, :8] = np.random.permutation(np.resize(levels, 8))
        for g in range(8):
            far = levels[np.abs(levels - a[p, g]) >= 10]
            a[p, g + 8] = far[np.random.randint(len(far))]
    return np.exp2(a.ravel()).repeat(32)


def f64(x):
    return np.asarray(x).astype(np.float64)


def striped(idx):
    return np.tile(idx.reshape(-1, 16).T, (8, 1)).astype(np.uint16)


def unstriped(offs):
    return offs[:16].T.reshape(-1).astype(np.int64)


def pack_weight(w):
    k, n = w.shape
    w = f64(np.asarray(w, np.float32).astype(ml_dtypes.bfloat16)).reshape(k // 32, 32, n)
    amax = np.abs(w).max(1)
    byte = np.clip(np.where(amax > 0, np.frexp(amax)[1] - 1 + 127 - 7, 1), 1, 254)
    scaled = (w * np.exp2(127.0 - byte)[:, None, :]).reshape(k, n).astype(np.float32)
    words = np.ascontiguousarray(scaled.reshape(k // 512, 128, 4, n).transpose(0, 1, 3, 2)).astype(ml_dtypes.float8_e4m3fn).view(np.uint8)
    return words, np.ascontiguousarray(byte.astype(np.uint8).reshape(k // 512, 16, n))


def unpack_weight(words, scales):
    g, p, n, _ = words.shape
    vals = np.ascontiguousarray(words).view(ml_dtypes.float8_e4m3fn).astype(np.float64) * np.repeat(np.exp2(scales.astype(np.float64) - 127.0), 8, axis=1)[..., None]
    return vals.transpose(0, 1, 3, 2).reshape(g * 512, n)


def silu(v):
    return v / (1.0 + np.exp(-np.maximum(v, -700.0)))


K, T, S, V, H, N, J, U = 512, 2048, 1024, 512, 512, 128, 512, 1024


def setup_inputs():
    n = np.random.standard_normal
    s = mx_kscale(K)[:, None]
    u = mx_kscale(H)
    r = mx_kscale(J)[:, None]
    packed_xT = pack_weight(n((K, T)) * s)
    return {
        "x_words": packed_xT[0],
        "x_scales": packed_xT[1],
        "aT": (n((J, U)) * r).astype(np.float32),
        "w1": (n((K, H)) / np.sqrt(K) / s * u).astype(np.float32),
        "w3": (n((J, H)) / np.sqrt(J) / r).astype(np.float32),
        "w2": (n((H, N)) / np.sqrt(2 * H) / u[:, None]).astype(np.float32),
        "offs": striped(np.random.permutation(T)[:S]),
        "pos1": striped(np.random.permutation(S)[:V]),
        "pos2": striped(np.random.permutation(S)[:V]),
    }


def reference(x_words, x_scales, aT, w1, w3, w2, offs, pos1, pos2):
    xq = unpack_weight(x_words, x_scales)[:, unstriped(offs)]
    h = silu(mxq(f64(w1), 0, "e4m3").T @ xq)
    f = mxq(f64(w3), 0, "e4m3").T @ mxq(f64(aT), 0, "e4m3")
    z = h[:, unstriped(pos1)] * f[:, :V] + h[:, unstriped(pos2)] * f[:, V:2 * V]
    return mxq(f64(w2), 0, "e4m3").T @ mxq(z, 0, "e4m3")

@@ -1,0 +1,210 @@
+from contextlib import ExitStack
+
+import concourse.mybir as mybir
+
+K, T, S, V, H, N, J = 512, 2048, 1024, 512, 512, 128, 512
+FLOPS = 2 * (K * H * S + J * H * S + H * N * V)
+
+F32 = mybir.dt.float32
+BF16 = mybir.dt.bfloat16
+I32 = mybir.dt.int32
+U32 = mybir.dt.uint32
+U16 = mybir.dt.uint16
+U8 = mybir.dt.uint8
+FP8X4 = mybir.dt.float8_e4m3fn_x4
+MULT = mybir.AluOpType.mult
+ADD = mybir.AluOpType.add
+SILU = mybir.ActivationFunctionType.Silu
+
+P = 128
+PACK = 4
+BANK = 512
+
+
+def tile_picked_dime_none_p_kernel(
+    tc, x_words, x_scales, aT, w1, w3, w2, offs, pos1, pos2, out
+):
+    nc = tc.nc
+    with ExitStack() as ctx:
+        keep = ctx.enter_context(tc.tile_pool(name="keep", bufs=1))
+        psum = ctx.enter_context(tc.psum_pool(name="psum", bufs=1))
+
+        def sb(name, shape, dtype):
+            return keep.tile(shape, dtype, name=name, align_bytes=64)
+
+        offs_sb = sb("offs_sb", [P, S // 16], U16)
+        pos_sb = [sb("pos1_sb", [P, V // 16], U16), sb("pos2_sb", [P, V // 16], U16)]
+        scale_win = sb("scale_win", [P, T], U8)
+        word_win = sb("word_win", [P, T], I32)
+        w1_raw = sb("w1_raw", [P, PACK, H], F32)
+        w3_raw = sb("w3_raw", [P, PACK, H], F32)
+        w2_raw = sb("w2_raw", [P, PACK, N], F32)
+        chunks = [(0, 256), (256, 256), (512, 512)]
+        a_raw = [sb(f"a_raw{c}", [P, PACK, w], F32) for c, (c0, w) in enumerate(chunks)]
+
+        warm_in = sb("warm_in", [P, 1], F32)
+        warm_out = sb("warm_out", [P, 1], F32)
+        nc.vector.memset(scale_win[:, 0:1280].bitcast(I32), 0)
+        nc.gpsimd.memset(scale_win[:, 1280:T].bitcast(I32), 0)
+        nc.vector.memset(warm_in[:], 0.0)
+
+        nc.sync.dma_start(offs_sb[:], offs)
+        nc.sync.dma_start(pos_sb[0][:], pos1)
+        nc.sync.dma_start(pos_sb[1][:], pos2)
+        for q in range(4):
+            nc.sync.dma_start(
+                scale_win[32 * q : 32 * q + 4, :].bitcast(I32),
+                x_scales[0, 4 * q : 4 * q + 4, :].bitcast(I32),
+            )
+        nc.scalar.activation(warm_out[:], warm_in[:], SILU)
+        nc.sync.dma_start(w1_raw[:], w1.rearrange("(p j) c -> p j c", j=PACK))
+        nc.sync.dma_start(word_win[:], x_words[0].rearrange("p n t -> p (n t)").bitcast(I32))
+        nc.sync.dma_start(w3_raw[:], w3.rearrange("(p j) c -> p j c", j=PACK))
+        a_rows = aT.rearrange("(p j) c -> p j c", j=PACK)
+
+        def load_a(c):
+            c0, w = chunks[c]
+            nc.sync.dma_start(a_raw[c][:], a_rows[:, :, c0 : c0 + w])
+
+        load_a(0)
+        load_a(1)
+        load_a(2)
+        nc.sync.dma_start(w2_raw[:], w2.rearrange("(p j) c -> p j c", j=PACK))
+
+        def copy_on(engine, dst, src):
+            if engine == "vector":
+                nc.vector.tensor_copy(dst, src)
+            else:
+                nc.scalar.copy(dst, src)
+
+        def quantize(name, grouped, width):
+            codes = sb(name + "_codes", [P, width], U32)
+            scales = sb(name + "_scales", [P, width], U8)
+            nc.vector.quantize_mx(out=codes[:].bitcast(FP8X4), scales=scales[:], in_=grouped[:])
+            return codes, scales
+
+        def group_weight_pair(name, raw, u, engine):
+            grouped = sb(name + "_grouped", [P, 2 * P * PACK], BF16)
+            dst = grouped[:].rearrange("p (e m j) -> p m j e", e=2, j=PACK)
+            src = raw[:].rearrange("p j (m t) -> p m j t", t=PACK)[:, :, :, 2 * u : 2 * u + 2]
+            copy_on(engine, dst, src)
+            return grouped
+
+        def group_columns(name, raw, width, engine):
+            grouped = sb(name + "_grouped", [P, width * PACK], BF16)
+            dst = grouped[:].rearrange("p (c i j) -> p c j i", i=4, j=PACK)
+            src = raw[:].rearrange("p j (c i) -> p c j i", i=4)
+            copy_on(engine, dst, src)
+            return grouped
+
+        def mm(dst, lhs, lhs_cols, rhs, rhs_cols):
+            nc.tensor.matmul_mx(
+                out=dst,
+                lhsT=lhs[0][:, lhs_cols].bitcast(FP8X4),
+                lhsT_scale=lhs[1][:, lhs_cols],
+                rhs=rhs[0][:, rhs_cols].bitcast(FP8X4),
+                rhs_scale=rhs[1][:, rhs_cols],
+                start=True,
+                stop=True,
+            )
+
+        x_scale = sb("x_scale", [P, S], U8)
+        nc.vector.tensor_copy(x_scale[:], scale_win[:].indirect(offs_sb[:]))
+        g0 = group_weight_pair("w1a", w1_raw, 0, "scalar")
+        g1 = group_weight_pair("w1b", w1_raw, 1, "scalar")
+        w1q = [quantize("w1a", g0, 2 * P), quantize("w1b", g1, 2 * P)]
+        x_code = []
+        for b in range(2):
+            xc = sb(f"x_code{b}", [P, BANK], U32)
+            nc.vector.tensor_copy(
+                xc[:], word_win[:].bitcast(U32).indirect(offs_sb[:, 32 * b : 32 * b + 32])
+            )
+            x_code.append(xc)
+
+        h = [sb(f"h{t}", [P, S], F32) for t in range(PACK)]
+
+        def make_h(t):
+            cols = slice((t % 2) * P, (t % 2 + 1) * P)
+            for b in range(2):
+                bank = psum.tile([P, BANK], F32, name="h_bank", bufs=4)
+                nc.tensor.matmul_mx(
+                    out=bank[:],
+                    lhsT=w1q[t // 2][0][:, cols].bitcast(FP8X4),
+                    lhsT_scale=w1q[t // 2][1][:, cols],
+                    rhs=x_code[b][:].bitcast(FP8X4),
+                    rhs_scale=x_scale[:, b * BANK : (b + 1) * BANK],
+                    start=True,
+                    stop=True,
+                )
+                nc.scalar.activation(h[t][:, b * BANK : (b + 1) * BANK], bank[:], SILU)
+
+        prod = [sb(f"prod{d}", [P, PACK, V], F32) for d in range(2)]
+        w3q = [None, None]
+        aq = [None, None, None]
+
+        def filters(c, tiles):
+            c0, w = chunks[c]
+            bank = psum.tile([P, BANK], F32, name="f_bank", bufs=3)
+            for n, t in enumerate(tiles):
+                mm(bank[:, n * w : (n + 1) * w], w3q[t // 2], slice((t % 2) * P, (t % 2 + 1) * P), aq[c], slice(0, w))
+            f = sb(f"f{c}_{tiles[0]}", [P, BANK], F32)
+            nc.scalar.copy(f[:], bank[:])
+            return f
+
+        def messages(c, tiles, f):
+            c0, w = chunks[c]
+            d, v0 = divmod(c0, V)
+            for n, t in enumerate(tiles):
+                nc.vector.tensor_tensor(
+                    prod[d][:, t, v0 : v0 + w],
+                    h[t][:].indirect(pos_sb[d][:, v0 // 16 : (v0 + w) // 16]),
+                    f[:, n * w : (n + 1) * w],
+                    MULT,
+                )
+
+        make_h(0)
+        make_h(1)
+        ga = group_weight_pair("w3a", w3_raw, 0, "vector")
+        gb = group_columns("a0", a_raw[0], 256, "vector")
+        w3q[0] = quantize("w3a", ga, 2 * P)
+        aq[0] = quantize("a0", gb, 256)
+        f_00 = filters(0, [0, 1])
+        gc = group_weight_pair("w3b", w3_raw, 1, "vector")
+        w3q[1] = quantize("w3b", gc, 2 * P)
+        make_h(2)
+        f_02 = filters(0, [2, 3])
+        make_h(3)
+        gd = group_columns("a1", a_raw[1], 256, "scalar")
+        messages(0, [0, 1], f_00)
+        aq[1] = quantize("a1", gd, 256)
+        f_10 = filters(1, [0, 1])
+        f_12 = filters(1, [2, 3])
+        ge = group_columns("a2", a_raw[2], 512, "scalar")
+        messages(0, [2, 3], f_02)
+        messages(1, [0, 1], f_10)
+        aq[2] = quantize("a2", ge, 512)
+        f_2 = [filters(2, [t]) for t in range(PACK)]
+        gw = group_columns("w2", w2_raw, N, "scalar")
+        messages(1, [2, 3], f_12)
+        for t in range(PACK):
+            messages(2, [t], f_2[t])
+        w2q = quantize("w2", gw, N)
+
+        half = V // 2
+        zs = []
+        for u in range(2):
+            z = sb(f"z{u}", [P, half * PACK], BF16)
+            nc.vector.tensor_tensor(
+                z[:].rearrange("p (c i j) -> p c j i", i=4, j=PACK),
+                prod[0][:, :, u * half : (u + 1) * half].rearrange("p j (c i) -> p c j i", i=4),
+                prod[1][:, :, u * half : (u + 1) * half].rearrange("p j (c i) -> p c j i", i=4),
+                ADD,
+            )
+            zs.append(z)
+        for u in range(2):
+            zq = quantize(f"z{u}", zs[u], half)
+            bank = psum.tile([P, BANK], F32, name="f_bank", bufs=3)
+            mm(bank[:, 0:half], w2q, slice(0, N), zq, slice(0, half))
+            res = sb(f"res{u}", [P, half], F32)
+            nc.scalar.copy(res[:], bank[:, 0:half])
+            nc.sync.dma_start(out[:, u * half : (u + 1) * half], res[:])

@@ -1,6 +1,7 @@
 from contextlib import ExitStack
 
 import concourse.mybir as mybir
+from concourse.masks import make_identity
 
 K, T, S, V, H, N, J = 512, 2048, 1024, 512, 512, 128, 512
 FLOPS = 2 * (K * H * S + J * H * S + H * N * V)
@@ -19,6 +20,7 @@ SILU = mybir.ActivationFunctionType.Silu
 P = 128
 PACK = 4
 BANK = 512
+HALF = V // 2
 
 
 def tile_picked_dime_none_p_kernel(
@@ -29,8 +31,8 @@ def tile_picked_dime_none_p_kernel(
         keep = ctx.enter_context(tc.tile_pool(name="keep", bufs=1))
         psum = ctx.enter_context(tc.psum_pool(name="psum", bufs=1))
 
-        def sb(name, shape, dtype):
-            return keep.tile(shape, dtype, name=name, align_bytes=64)
+        def sb(name, shape, dtype, tag=""):
+            return keep.tile(shape, dtype, name=name, tag=tag or name, align_bytes=64)
 
         offs_sb = sb("offs_sb", [P, S // 16], U16)
         pos_sb = [sb("pos1_sb", [P, V // 16], U16), sb("pos2_sb", [P, V // 16], U16)]
@@ -39,14 +41,17 @@ def tile_picked_dime_none_p_kernel(
         w1_raw = sb("w1_raw", [P, PACK, H], F32)
         w3_raw = sb("w3_raw", [P, PACK, H], F32)
         w2_raw = sb("w2_raw", [P, PACK, N], F32)
-        chunks = [(0, 256), (256, 256), (512, 512)]
-        a_raw = [sb(f"a_raw{c}", [P, PACK, w], F32) for c, (c0, w) in enumerate(chunks)]
+        chunks = [(0, 0), (1, 0), (0, 1), (1, 1)]
+        a_raw = [sb(f"a_raw{c}", [P, PACK, HALF], F32) for c in range(4)]
 
         warm_in = sb("warm_in", [P, 1], F32)
         warm_out = sb("warm_out", [P, 1], F32)
         nc.vector.memset(scale_win[:, 0:1280].bitcast(I32), 0)
         nc.gpsimd.memset(scale_win[:, 1280:T].bitcast(I32), 0)
         nc.vector.memset(warm_in[:], 0.0)
+        nc.scalar.activation(warm_out[:], warm_in[:], SILU)
+        ident = sb("ident", [P, P], F32)
+        make_identity(nc, ident[:])
 
         nc.sync.dma_start(offs_sb[:], offs)
         nc.sync.dma_start(pos_sb[0][:], pos1)
@@ -56,63 +61,61 @@ def tile_picked_dime_none_p_kernel(
                 scale_win[32 * q : 32 * q + 4, :].bitcast(I32),
                 x_scales[0, 4 * q : 4 * q + 4, :].bitcast(I32),
             )
-        nc.scalar.activation(warm_out[:], warm_in[:], SILU)
-        nc.sync.dma_start(w1_raw[:], w1.rearrange("(p j) c -> p j c", j=PACK))
-        nc.sync.dma_start(word_win[:], x_words[0].rearrange("p n t -> p (n t)").bitcast(I32))
-        nc.sync.dma_start(w3_raw[:], w3.rearrange("(p j) c -> p j c", j=PACK))
         a_rows = aT.rearrange("(p j) c -> p j c", j=PACK)
 
         def load_a(c):
-            c0, w = chunks[c]
-            nc.sync.dma_start(a_raw[c][:], a_rows[:, :, c0 : c0 + w])
+            d, u = chunks[c]
+            c0 = d * V + u * HALF
+            nc.sync.dma_start(a_raw[c][:], a_rows[:, :, c0 : c0 + HALF])
 
+        nc.sync.dma_start(word_win[:], x_words[0].rearrange("p n t -> p (n t)").bitcast(I32))
+        nc.sync.dma_start(w1_raw[:], w1.rearrange("(p j) c -> p j c", j=PACK))
         load_a(0)
+        nc.sync.dma_start(w3_raw[:], w3.rearrange("(p j) c -> p j c", j=PACK))
         load_a(1)
         load_a(2)
+        load_a(3)
         nc.sync.dma_start(w2_raw[:], w2.rearrange("(p j) c -> p j c", j=PACK))
 
-        def copy_on(engine, dst, src):
-            if engine == "vector":
-                nc.vector.tensor_copy(dst, src)
-            else:
-                nc.scalar.copy(dst, src)
-
-        def quantize(name, grouped, width):
-            codes = sb(name + "_codes", [P, width], U32)
+        def quantize(name, grouped, width, tag=""):
+            codes = sb(name + "_codes", [P, width], U32, tag)
             scales = sb(name + "_scales", [P, width], U8)
             nc.vector.quantize_mx(out=codes[:].bitcast(FP8X4), scales=scales[:], in_=grouped[:])
             return codes, scales
 
-        def group_weight_pair(name, raw, u, engine):
+        def group_weight_pair(name, raw, u, copy):
             grouped = sb(name + "_grouped", [P, 2 * P * PACK], BF16)
             dst = grouped[:].rearrange("p (e m j) -> p m j e", e=2, j=PACK)
             src = raw[:].rearrange("p j (m t) -> p m j t", t=PACK)[:, :, :, 2 * u : 2 * u + 2]
-            copy_on(engine, dst, src)
+            copy(dst, src)
             return grouped
 
-        def group_columns(name, raw, width, engine):
-            grouped = sb(name + "_grouped", [P, width * PACK], BF16)
+        def group_columns(name, raw, width, copy, tag=""):
+            grouped = sb(name + "_grouped", [P, width * PACK], BF16, tag)
             dst = grouped[:].rearrange("p (c i j) -> p c j i", i=4, j=PACK)
             src = raw[:].rearrange("p j (c i) -> p c j i", i=4)
-            copy_on(engine, dst, src)
+            copy(dst, src)
             return grouped
 
-        def mm(dst, lhs, lhs_cols, rhs, rhs_cols):
+        def mm(dst, lhs, lhs_cols, rhs_codes, rhs_scales):
             nc.tensor.matmul_mx(
                 out=dst,
                 lhsT=lhs[0][:, lhs_cols].bitcast(FP8X4),
                 lhsT_scale=lhs[1][:, lhs_cols],
-                rhs=rhs[0][:, rhs_cols].bitcast(FP8X4),
-                rhs_scale=rhs[1][:, rhs_cols],
+                rhs=rhs_codes.bitcast(FP8X4),
+                rhs_scale=rhs_scales,
                 start=True,
                 stop=True,
             )
 
+        def new_bank():
+            return psum.tile([P, BANK], F32, name="bank", bufs=5)
+
+        on_vector = nc.vector.tensor_copy
+        on_scalar = nc.scalar.copy
+
         x_scale = sb("x_scale", [P, S], U8)
         nc.vector.tensor_copy(x_scale[:], scale_win[:].indirect(offs_sb[:]))
-        g0 = group_weight_pair("w1a", w1_raw, 0, "scalar")
-        g1 = group_weight_pair("w1b", w1_raw, 1, "scalar")
-        w1q = [quantize("w1a", g0, 2 * P), quantize("w1b", g1, 2 * P)]
         x_code = []
         for b in range(2):
             xc = sb(f"x_code{b}", [P, BANK], U32)
@@ -121,90 +124,126 @@ def tile_picked_dime_none_p_kernel(
             )
             x_code.append(xc)
 
+        g0 = group_weight_pair("w1a", w1_raw, 0, on_vector)
+        g1 = group_weight_pair("w1b", w1_raw, 1, on_scalar)
+        w1q = [quantize("w1a", g0, 2 * P), quantize("w1b", g1, 2 * P)]
+
         h = [sb(f"h{t}", [P, S], F32) for t in range(PACK)]
 
-        def make_h(t):
-            cols = slice((t % 2) * P, (t % 2 + 1) * P)
-            for b in range(2):
-                bank = psum.tile([P, BANK], F32, name="h_bank", bufs=4)
-                nc.tensor.matmul_mx(
-                    out=bank[:],
-                    lhsT=w1q[t // 2][0][:, cols].bitcast(FP8X4),
-                    lhsT_scale=w1q[t // 2][1][:, cols],
-                    rhs=x_code[b][:].bitcast(FP8X4),
-                    rhs_scale=x_scale[:, b * BANK : (b + 1) * BANK],
-                    start=True,
-                    stop=True,
-                )
-                nc.scalar.activation(h[t][:, b * BANK : (b + 1) * BANK], bank[:], SILU)
+        def make_h(t, b):
+            cols = slice(b * BANK, (b + 1) * BANK)
+            bank = new_bank()
+            mm(bank[:], w1q[t // 2], slice((t % 2) * P, (t % 2 + 1) * P), x_code[b][:], x_scale[:, cols])
+            nc.scalar.activation(h[t][:, cols], bank[:], SILU)
 
-        prod = [sb(f"prod{d}", [P, PACK, V], F32) for d in range(2)]
+        prod = [sb(f"prod{c}", [P, PACK, HALF], F32) for c in range(4)]
         w3q = [None, None]
-        aq = [None, None, None]
+        aq = [None] * 4
+        f = {}
 
-        def filters(c, tiles):
-            c0, w = chunks[c]
-            bank = psum.tile([P, BANK], F32, name="f_bank", bufs=3)
-            for n, t in enumerate(tiles):
-                mm(bank[:, n * w : (n + 1) * w], w3q[t // 2], slice((t % 2) * P, (t % 2 + 1) * P), aq[c], slice(0, w))
-            f = sb(f"f{c}_{tiles[0]}", [P, BANK], F32)
-            nc.scalar.copy(f[:], bank[:])
-            return f
+        def filters(c, pair):
+            bank = new_bank()
+            for e in range(2):
+                mm(bank[:, e * HALF : (e + 1) * HALF], w3q[pair], slice(e * P, (e + 1) * P), aq[c][0][:], aq[c][1][:])
+            f[c, pair] = sb(f"f{c}_{pair}", [P, BANK], F32)
+            nc.scalar.copy(f[c, pair][:], bank[:])
 
-        def messages(c, tiles, f):
-            c0, w = chunks[c]
-            d, v0 = divmod(c0, V)
-            for n, t in enumerate(tiles):
+        def messages(c, pair):
+            d, u = chunks[c]
+            for e in range(2):
+                t = 2 * pair + e
                 nc.vector.tensor_tensor(
-                    prod[d][:, t, v0 : v0 + w],
-                    h[t][:].indirect(pos_sb[d][:, v0 // 16 : (v0 + w) // 16]),
-                    f[:, n * w : (n + 1) * w],
+                    prod[c][:, t, :],
+                    h[t][:].indirect(pos_sb[d][:, u * 16 : (u + 1) * 16]),
+                    f[c, pair][:, e * HALF : (e + 1) * HALF],
                     MULT,
                 )
 
-        make_h(0)
-        make_h(1)
-        ga = group_weight_pair("w3a", w3_raw, 0, "vector")
-        gb = group_columns("a0", a_raw[0], 256, "vector")
-        w3q[0] = quantize("w3a", ga, 2 * P)
-        aq[0] = quantize("a0", gb, 256)
-        f_00 = filters(0, [0, 1])
-        gc = group_weight_pair("w3b", w3_raw, 1, "vector")
-        w3q[1] = quantize("w3b", gc, 2 * P)
-        make_h(2)
-        f_02 = filters(0, [2, 3])
-        make_h(3)
-        gd = group_columns("a1", a_raw[1], 256, "scalar")
-        messages(0, [0, 1], f_00)
-        aq[1] = quantize("a1", gd, 256)
-        f_10 = filters(1, [0, 1])
-        f_12 = filters(1, [2, 3])
-        ge = group_columns("a2", a_raw[2], 512, "scalar")
-        messages(0, [2, 3], f_02)
-        messages(1, [0, 1], f_10)
-        aq[2] = quantize("a2", ge, 512)
-        f_2 = [filters(2, [t]) for t in range(PACK)]
-        gw = group_columns("w2", w2_raw, N, "scalar")
-        messages(1, [2, 3], f_12)
-        for t in range(PACK):
-            messages(2, [t], f_2[t])
-        w2q = quantize("w2", gw, N)
-
-        half = V // 2
-        zs = []
-        for u in range(2):
-            z = sb(f"z{u}", [P, half * PACK], BF16)
+        def sum_on_vector(u):
+            z = sb(f"z{u}", [P, HALF * PACK], BF16)
             nc.vector.tensor_tensor(
                 z[:].rearrange("p (c i j) -> p c j i", i=4, j=PACK),
-                prod[0][:, :, u * half : (u + 1) * half].rearrange("p j (c i) -> p c j i", i=4),
-                prod[1][:, :, u * half : (u + 1) * half].rearrange("p j (c i) -> p c j i", i=4),
+                prod[2 * u][:].rearrange("p j (c i) -> p c j i", i=4),
+                prod[2 * u + 1][:].rearrange("p j (c i) -> p c j i", i=4),
                 ADD,
             )
-            zs.append(z)
-        for u in range(2):
-            zq = quantize(f"z{u}", zs[u], half)
-            bank = psum.tile([P, BANK], F32, name="f_bank", bufs=3)
-            mm(bank[:, 0:half], w2q, slice(0, N), zq, slice(0, half))
-            res = sb(f"res{u}", [P, half], F32)
-            nc.scalar.copy(res[:], bank[:, 0:half])
-            nc.sync.dma_start(out[:, u * half : (u + 1) * half], res[:])
+            return z
+
+        def sum_on_tensor(u):
+            turned = []
+            for vb in range(2):
+                bank = psum.tile([P, BANK], F32, name="turn_bank", bufs=3)
+                for t in range(PACK):
+                    for d in range(2):
+                        nc.tensor.matmul(
+                            bank[:, t * P : (t + 1) * P],
+                            lhsT=prod[2 * u + d][:, t, vb * P : (vb + 1) * P],
+                            rhs=ident[:],
+                            is_transpose=True,
+                            start=(d == 0),
+                            stop=(d == 1),
+                        )
+                zt = sb(f"zt{u}_{vb}", [P, H], BF16)
+                nc.scalar.copy(
+                    zt[:].rearrange("v (w m e) -> v w m e", w=2, e=2),
+                    bank[:].rearrange("v (w e m) -> v w m e", w=2, e=2),
+                )
+                turned.append(zt)
+            bank = psum.tile([P, BANK], F32, name="turn_bank", bufs=3)
+            for vb in range(2):
+                words = turned[vb][:].bitcast(F32)
+                for w in range(2):
+                    col = (2 * vb + w) * P
+                    nc.tensor.transpose(bank[:, col : col + P], words[:, w * P : (w + 1) * P], ident[:])
+            z = sb(f"z{u}", [P, HALF * PACK], BF16)
+            nc.scalar.copy(
+                z[:].bitcast(F32).rearrange("p (b v w) -> p b v w", b=2, w=2),
+                bank[:].rearrange("p (b w v) -> p b v w", b=2, w=2),
+            )
+            return z
+
+        def project(u, z):
+            zq = quantize(f"z{u}", z, HALF, "z0" if u == 1 else "")
+            bank = new_bank()
+            mm(bank[:, 0:HALF], w2q, slice(0, N), zq[0][:], zq[1][:])
+            res = sb(f"res{u}", [P, HALF], F32)
+            nc.scalar.copy(res[:], bank[:, 0:HALF])
+            nc.sync.dma_start(out[:, u * HALF : (u + 1) * HALF], res[:])
+
+        make_h(0, 0)
+        make_h(0, 1)
+        make_h(1, 0)
+        make_h(1, 1)
+        aq[0] = quantize("a0", group_columns("a0", a_raw[0], HALF, on_vector), HALF)
+        ga = group_weight_pair("w3a", w3_raw, 0, on_vector)
+        gb = group_weight_pair("w3b", w3_raw, 1, on_vector)
+        w3q[0] = quantize("w3a", ga, 2 * P)
+        w3q[1] = quantize("w3b", gb, 2 * P)
+        make_h(2, 0)
+        filters(0, 0)
+        aq[1] = quantize("a1", group_columns("a1", a_raw[1], HALF, on_vector), HALF)
+        make_h(2, 1)
+        filters(1, 0)
+        filters(0, 1)
+        make_h(3, 0)
+        make_h(3, 1)
+        messages(0, 0)
+        messages(1, 0)
+        messages(0, 1)
+        aq[2] = quantize("a2", group_columns("a2", a_raw[2], HALF, on_scalar, "f0_0"), HALF)
+        filters(1, 1)
+        messages(1, 1)
+        aq[3] = quantize("a3", group_columns("a3", a_raw[3], HALF, on_scalar, "f1_0"), HALF)
+        filters(2, 0)
+        filters(2, 1)
+        gw = group_columns("w2", w2_raw, N, on_scalar)
+        filters(3, 0)
+        filters(3, 1)
+        z0 = sum_on_tensor(0)
+        messages(2, 0)
+        messages(2, 1)
+        w2q = quantize("w2", gw, N)
+        project(0, z0)
+        messages(3, 0)
+        messages(3, 1)
+        project(1, sum_on_vector(1))

@@ -54,6 +54,7 @@ def tile_picked_dime_none_p_kernel(
         make_identity(nc, ident[:])
 
         nc.sync.dma_start(offs_sb[:], offs)
+        nc.sync.dma_start(word_win[:], x_words[0].rearrange("p n t -> p (n t)").bitcast(I32))
         nc.sync.dma_start(pos_sb[0][:], pos1)
         nc.sync.dma_start(pos_sb[1][:], pos2)
         for q in range(4):
@@ -68,7 +69,6 @@ def tile_picked_dime_none_p_kernel(
             c0 = d * V + u * HALF
             nc.sync.dma_start(a_raw[c][:], a_rows[:, :, c0 : c0 + HALF])
 
-        nc.sync.dma_start(word_win[:], x_words[0].rearrange("p n t -> p (n t)").bitcast(I32))
         nc.sync.dma_start(w1_raw[:], w1.rearrange("(p j) c -> p j c", j=PACK))
         load_a(0)
         nc.sync.dma_start(w3_raw[:], w3.rearrange("(p j) c -> p j c", j=PACK))
@@ -114,26 +114,31 @@ def tile_picked_dime_none_p_kernel(
         on_vector = nc.vector.tensor_copy
         on_scalar = nc.scalar.copy
 
-        x_scale = sb("x_scale", [P, S], U8)
-        nc.vector.tensor_copy(x_scale[:], scale_win[:].indirect(offs_sb[:]))
-        x_code = []
-        for b in range(2):
-            xc = sb(f"x_code{b}", [P, BANK], U32)
-            nc.vector.tensor_copy(
-                xc[:], word_win[:].bitcast(U32).indirect(offs_sb[:, 32 * b : 32 * b + 32])
-            )
-            x_code.append(xc)
+        def pick_words(b):
+            picked = sb(f"x_code{b}", [P, BANK], U32)
+            nc.vector.tensor_copy(picked[:], word_win[:].bitcast(U32).indirect(offs_sb[:, 32 * b : 32 * b + 32]))
+            return picked
 
-        g0 = group_weight_pair("w1a", w1_raw, 0, on_vector)
+        def pick_scales(b, tag=""):
+            picked = sb(f"x_scale{b}", [P, BANK], U8, tag)
+            nc.vector.tensor_copy(picked[:], scale_win[:].indirect(offs_sb[:, 32 * b : 32 * b + 32]))
+            return picked
+
+        x_code = [pick_words(0)]
+        x_scale = [pick_scales(0)]
+        x_code.append(pick_words(1))
+        g0 = group_weight_pair("w1a", w1_raw, 0, on_scalar)
         g1 = group_weight_pair("w1b", w1_raw, 1, on_scalar)
-        w1q = [quantize("w1a", g0, 2 * P), quantize("w1b", g1, 2 * P)]
+        w1q = [quantize("w1a", g0, 2 * P)]
+        x_scale.append(pick_scales(1, "w1a_grouped"))
+        w1q.append(quantize("w1b", g1, 2 * P))
 
         h = [sb(f"h{t}", [P, S], F32) for t in range(PACK)]
 
         def make_h(t, b):
             cols = slice(b * BANK, (b + 1) * BANK)
             bank = new_bank()
-            mm(bank[:], w1q[t // 2], slice((t % 2) * P, (t % 2 + 1) * P), x_code[b][:], x_scale[:, cols])
+            mm(bank[:], w1q[t // 2], slice((t % 2) * P, (t % 2 + 1) * P), x_code[b][:], x_scale[b][:])
             nc.scalar.activation(h[t][:, cols], bank[:], SILU)
 
         prod = [sb(f"prod{c}", [P, PACK, HALF], F32) for c in range(4)]
@@ -210,12 +215,13 @@ def tile_picked_dime_none_p_kernel(
             nc.scalar.copy(res[:], bank[:, 0:HALF])
             nc.sync.dma_start(out[:, u * HALF : (u + 1) * HALF], res[:])
 
+        g_a0 = group_columns("a0", a_raw[0], HALF, on_scalar)
         make_h(0, 0)
-        make_h(0, 1)
         make_h(1, 0)
+        make_h(0, 1)
         make_h(1, 1)
-        aq[0] = quantize("a0", group_columns("a0", a_raw[0], HALF, on_vector), HALF)
         ga = group_weight_pair("w3a", w3_raw, 0, on_vector)
+        aq[0] = quantize("a0", g_a0, HALF)
         gb = group_weight_pair("w3b", w3_raw, 1, on_vector)
         w3q[0] = quantize("w3a", ga, 2 * P)
         w3q[1] = quantize("w3b", gb, 2 * P)

@@ -19,8 +19,14 @@ SILU = mybir.ActivationFunctionType.Silu
 
 P = 128
 PACK = 4
+LINE = 4
+GROUP = 16
 BANK = 512
 HALF = V // 2
+PRODUCT_BANKS = 5
+TURN_BANKS = 3
+
+CHUNKS = [(d, u) for u in range(2) for d in range(2)]
 
 
 def tile_picked_dime_none_p_kernel(
@@ -31,225 +37,232 @@ def tile_picked_dime_none_p_kernel(
         keep = ctx.enter_context(tc.tile_pool(name="keep", bufs=1))
         psum = ctx.enter_context(tc.psum_pool(name="psum", bufs=1))
 
-        def sb(name, shape, dtype, tag=""):
-            return keep.tile(shape, dtype, name=name, tag=tag or name, align_bytes=64)
+        def sbuf(name, shape, dtype, reuses=""):
+            return keep.tile(shape, dtype, name=name, tag=reuses or name, align_bytes=64)
 
-        offs_sb = sb("offs_sb", [P, S // 16], U16)
-        pos_sb = [sb("pos1_sb", [P, V // 16], U16), sb("pos2_sb", [P, V // 16], U16)]
-        scale_win = sb("scale_win", [P, T], U8)
-        word_win = sb("word_win", [P, T], I32)
-        w1_raw = sb("w1_raw", [P, PACK, H], F32)
-        w3_raw = sb("w3_raw", [P, PACK, H], F32)
-        w2_raw = sb("w2_raw", [P, PACK, N], F32)
-        chunks = [(0, 0), (1, 0), (0, 1), (1, 1)]
-        a_raw = [sb(f"a_raw{c}", [P, PACK, HALF], F32) for c in range(4)]
+        offs_sb = sbuf("offs_sb", [P, S // GROUP], U16)
+        pos_sb = [sbuf("pos1_sb", [P, V // GROUP], U16), sbuf("pos2_sb", [P, V // GROUP], U16)]
+        scale_table = sbuf("scale_table", [P, T], U8)
+        word_table = sbuf("word_table", [P, T], I32)
+        w1_raw = sbuf("w1_raw", [P, PACK, H], F32)
+        w3_raw = sbuf("w3_raw", [P, PACK, H], F32)
+        w2_raw = sbuf("w2_raw", [P, PACK, N], F32)
+        a_raw = [sbuf(f"a_raw{c}", [P, PACK, HALF], F32) for c in range(len(CHUNKS))]
 
-        warm_in = sb("warm_in", [P, 1], F32)
-        warm_out = sb("warm_out", [P, 1], F32)
-        nc.vector.memset(scale_win[:, 0:1280].bitcast(I32), 0)
-        nc.gpsimd.memset(scale_win[:, 1280:T].bitcast(I32), 0)
+        nc.vector.memset(scale_table[:].bitcast(I32), 0)
+
+        warm_in = sbuf("warm_in", [P, 1], F32)
+        warm_out = sbuf("warm_out", [P, 1], F32)
         nc.vector.memset(warm_in[:], 0.0)
         nc.scalar.activation(warm_out[:], warm_in[:], SILU)
-        ident = sb("ident", [P, P], F32)
-        make_identity(nc, ident[:])
+
+        identity = sbuf("identity", [P, P], F32)
+        make_identity(nc, identity[:])
+
+        a_rows = aT.rearrange("(p j) c -> p j c", j=PACK)
+
+        def load_chunk(c):
+            d, u = CHUNKS[c]
+            first = d * V + u * HALF
+            nc.sync.dma_start(a_raw[c][:], a_rows[:, :, first : first + HALF])
 
         nc.sync.dma_start(offs_sb[:], offs)
-        nc.sync.dma_start(word_win[:], x_words[0].rearrange("p n t -> p (n t)").bitcast(I32))
+        nc.sync.dma_start(word_table[:], x_words[0].rearrange("p n j -> p (n j)").bitcast(I32))
         nc.sync.dma_start(pos_sb[0][:], pos1)
         nc.sync.dma_start(pos_sb[1][:], pos2)
         for q in range(4):
             nc.sync.dma_start(
-                scale_win[32 * q : 32 * q + 4, :].bitcast(I32),
+                scale_table[32 * q : 32 * q + 4, :].bitcast(I32),
                 x_scales[0, 4 * q : 4 * q + 4, :].bitcast(I32),
             )
-        a_rows = aT.rearrange("(p j) c -> p j c", j=PACK)
-
-        def load_a(c):
-            d, u = chunks[c]
-            c0 = d * V + u * HALF
-            nc.sync.dma_start(a_raw[c][:], a_rows[:, :, c0 : c0 + HALF])
-
         nc.sync.dma_start(w1_raw[:], w1.rearrange("(p j) c -> p j c", j=PACK))
-        load_a(0)
+        load_chunk(0)
         nc.sync.dma_start(w3_raw[:], w3.rearrange("(p j) c -> p j c", j=PACK))
-        load_a(1)
-        load_a(2)
-        load_a(3)
+        for c in range(1, len(CHUNKS)):
+            load_chunk(c)
         nc.sync.dma_start(w2_raw[:], w2.rearrange("(p j) c -> p j c", j=PACK))
-
-        def quantize(name, grouped, width, tag=""):
-            codes = sb(name + "_codes", [P, width], U32, tag)
-            scales = sb(name + "_scales", [P, width], U8)
-            nc.vector.quantize_mx(out=codes[:].bitcast(FP8X4), scales=scales[:], in_=grouped[:])
-            return codes, scales
-
-        def group_weight_pair(name, raw, u, copy):
-            grouped = sb(name + "_grouped", [P, 2 * P * PACK], BF16)
-            dst = grouped[:].rearrange("p (e m j) -> p m j e", e=2, j=PACK)
-            src = raw[:].rearrange("p j (m t) -> p m j t", t=PACK)[:, :, :, 2 * u : 2 * u + 2]
-            copy(dst, src)
-            return grouped
-
-        def group_columns(name, raw, width, copy, tag=""):
-            grouped = sb(name + "_grouped", [P, width * PACK], BF16, tag)
-            dst = grouped[:].rearrange("p (c i j) -> p c j i", i=4, j=PACK)
-            src = raw[:].rearrange("p j (c i) -> p c j i", i=4)
-            copy(dst, src)
-            return grouped
-
-        def mm(dst, lhs, lhs_cols, rhs_codes, rhs_scales):
-            nc.tensor.matmul_mx(
-                out=dst,
-                lhsT=lhs[0][:, lhs_cols].bitcast(FP8X4),
-                lhsT_scale=lhs[1][:, lhs_cols],
-                rhs=rhs_codes.bitcast(FP8X4),
-                rhs_scale=rhs_scales,
-                start=True,
-                stop=True,
-            )
-
-        def new_bank():
-            return psum.tile([P, BANK], F32, name="bank", bufs=5)
 
         on_vector = nc.vector.tensor_copy
         on_scalar = nc.scalar.copy
 
+        def by_lines(rows):
+            return rows.rearrange("p j (c i) -> p c j i", i=LINE)
+
+        def side_by_side(grouped):
+            return grouped.rearrange("p (c i j) -> p c j i", i=LINE, j=PACK)
+
+        def group_columns(name, raw, width, copy, reuses=""):
+            grouped = sbuf(name + "_grouped", [P, width * PACK], BF16, reuses)
+            copy(side_by_side(grouped[:]), by_lines(raw[:]))
+            return grouped
+
+        def group_weight_pair(name, raw, pair, copy):
+            grouped = sbuf(name + "_grouped", [P, 2 * P * PACK], BF16)
+            copy(
+                grouped[:].rearrange("p (e m j) -> p m j e", e=2, j=PACK),
+                raw[:].rearrange("p j (m t) -> p m j t", t=PACK)[:, :, :, 2 * pair : 2 * pair + 2],
+            )
+            return grouped
+
+        def quantize(name, grouped, width, reuses=""):
+            words = sbuf(name + "_words", [P, width], U32, reuses)
+            scales = sbuf(name + "_scales", [P, width], U8)
+            nc.vector.quantize_mx(out=words[:].bitcast(FP8X4), scales=scales[:], in_=grouped[:])
+            return words, scales
+
+        def multiply(result, stationary, first, moving):
+            nc.tensor.matmul_mx(
+                out=result,
+                lhsT=stationary[0][:, first : first + P].bitcast(FP8X4),
+                lhsT_scale=stationary[1][:, first : first + P],
+                rhs=moving[0][:].bitcast(FP8X4),
+                rhs_scale=moving[1][:],
+                start=True,
+                stop=True,
+            )
+
+        def product_bank():
+            return psum.tile([P, BANK], F32, name="product_bank", bufs=PRODUCT_BANKS)
+
+        def turn_bank():
+            return psum.tile([P, BANK], F32, name="turn_bank", bufs=TURN_BANKS)
+
+        def picked_entries(b):
+            return offs_sb[:, b * BANK // GROUP : (b + 1) * BANK // GROUP]
+
         def pick_words(b):
-            picked = sb(f"x_code{b}", [P, BANK], U32)
-            nc.vector.tensor_copy(picked[:], word_win[:].bitcast(U32).indirect(offs_sb[:, 32 * b : 32 * b + 32]))
+            picked = sbuf(f"x_words{b}", [P, BANK], U32)
+            nc.vector.tensor_copy(picked[:], word_table[:].bitcast(U32).indirect(picked_entries(b)))
             return picked
 
-        def pick_scales(b, tag=""):
-            picked = sb(f"x_scale{b}", [P, BANK], U8, tag)
-            nc.vector.tensor_copy(picked[:], scale_win[:].indirect(offs_sb[:, 32 * b : 32 * b + 32]))
+        def pick_scales(b, reuses=""):
+            picked = sbuf(f"x_scales{b}", [P, BANK], U8, reuses)
+            nc.vector.tensor_copy(picked[:], scale_table[:].indirect(picked_entries(b)))
             return picked
 
-        x_code = [pick_words(0)]
-        x_scale = [pick_scales(0)]
-        x_code.append(pick_words(1))
-        g0 = group_weight_pair("w1a", w1_raw, 0, on_scalar)
-        g1 = group_weight_pair("w1b", w1_raw, 1, on_scalar)
-        w1q = [quantize("w1a", g0, 2 * P)]
-        x_scale.append(pick_scales(1, "w1a_grouped"))
-        w1q.append(quantize("w1b", g1, 2 * P))
-
-        h = [sb(f"h{t}", [P, S], F32) for t in range(PACK)]
+        h = [sbuf(f"h{t}", [P, S], F32) for t in range(PACK)]
+        products = [sbuf(f"products{c}", [P, PACK, HALF], F32) for c in range(len(CHUNKS))]
+        w1_q, w3_q, a_q, x_q, f = {}, {}, {}, {}, {}
 
         def make_h(t, b):
-            cols = slice(b * BANK, (b + 1) * BANK)
-            bank = new_bank()
-            mm(bank[:], w1q[t // 2], slice((t % 2) * P, (t % 2 + 1) * P), x_code[b][:], x_scale[b][:])
-            nc.scalar.activation(h[t][:, cols], bank[:], SILU)
+            bank = product_bank()
+            multiply(bank[:], w1_q[t // 2], (t % 2) * P, x_q[b])
+            nc.scalar.activation(h[t][:, b * BANK : (b + 1) * BANK], bank[:], SILU)
 
-        prod = [sb(f"prod{c}", [P, PACK, HALF], F32) for c in range(4)]
-        w3q = [None, None]
-        aq = [None] * 4
-        f = {}
-
-        def filters(c, pair):
-            bank = new_bank()
+        def make_f(c, pair):
+            bank = product_bank()
             for e in range(2):
-                mm(bank[:, e * HALF : (e + 1) * HALF], w3q[pair], slice(e * P, (e + 1) * P), aq[c][0][:], aq[c][1][:])
-            f[c, pair] = sb(f"f{c}_{pair}", [P, BANK], F32)
+                multiply(bank[:, e * HALF : (e + 1) * HALF], w3_q[pair], e * P, a_q[c])
+            f[c, pair] = sbuf(f"f{c}_{pair}", [P, BANK], F32)
             nc.scalar.copy(f[c, pair][:], bank[:])
 
-        def messages(c, pair):
-            d, u = chunks[c]
+        def gather_times_f(c, pair):
+            d, u = CHUNKS[c]
+            places = pos_sb[d][:, u * HALF // GROUP : (u + 1) * HALF // GROUP]
             for e in range(2):
                 t = 2 * pair + e
                 nc.vector.tensor_tensor(
-                    prod[c][:, t, :],
-                    h[t][:].indirect(pos_sb[d][:, u * 16 : (u + 1) * 16]),
+                    products[c][:, t, :],
+                    h[t][:].indirect(places),
                     f[c, pair][:, e * HALF : (e + 1) * HALF],
                     MULT,
                 )
 
         def sum_on_vector(u):
-            z = sb(f"z{u}", [P, HALF * PACK], BF16)
+            z = sbuf(f"z{u}", [P, HALF * PACK], BF16)
             nc.vector.tensor_tensor(
-                z[:].rearrange("p (c i j) -> p c j i", i=4, j=PACK),
-                prod[2 * u][:].rearrange("p j (c i) -> p c j i", i=4),
-                prod[2 * u + 1][:].rearrange("p j (c i) -> p c j i", i=4),
-                ADD,
+                side_by_side(z[:]), by_lines(products[2 * u][:]), by_lines(products[2 * u + 1][:]), ADD
             )
             return z
 
         def sum_on_tensor(u):
+            blocks = HALF // P
             turned = []
-            for vb in range(2):
-                bank = psum.tile([P, BANK], F32, name="turn_bank", bufs=3)
+            for block in range(blocks):
+                bank = turn_bank()
                 for t in range(PACK):
                     for d in range(2):
                         nc.tensor.matmul(
                             bank[:, t * P : (t + 1) * P],
-                            lhsT=prod[2 * u + d][:, t, vb * P : (vb + 1) * P],
-                            rhs=ident[:],
+                            lhsT=products[2 * u + d][:, t, block * P : (block + 1) * P],
+                            rhs=identity[:],
                             is_transpose=True,
                             start=(d == 0),
                             stop=(d == 1),
                         )
-                zt = sb(f"zt{u}_{vb}", [P, H], BF16)
+                z_turned = sbuf(f"z_turned{block}", [P, H], BF16)
                 nc.scalar.copy(
-                    zt[:].rearrange("v (w m e) -> v w m e", w=2, e=2),
+                    z_turned[:].rearrange("v (w m e) -> v w m e", w=2, e=2),
                     bank[:].rearrange("v (w e m) -> v w m e", w=2, e=2),
                 )
-                turned.append(zt)
-            bank = psum.tile([P, BANK], F32, name="turn_bank", bufs=3)
-            for vb in range(2):
-                words = turned[vb][:].bitcast(F32)
+                turned.append(z_turned)
+            bank = turn_bank()
+            for block in range(blocks):
+                pairs = turned[block][:].bitcast(F32)
                 for w in range(2):
-                    col = (2 * vb + w) * P
-                    nc.tensor.transpose(bank[:, col : col + P], words[:, w * P : (w + 1) * P], ident[:])
-            z = sb(f"z{u}", [P, HALF * PACK], BF16)
+                    first = (2 * block + w) * P
+                    nc.tensor.transpose(
+                        bank[:, first : first + P], pairs[:, w * P : (w + 1) * P], identity[:]
+                    )
+            z = sbuf(f"z{u}", [P, HALF * PACK], BF16)
             nc.scalar.copy(
-                z[:].bitcast(F32).rearrange("p (b v w) -> p b v w", b=2, w=2),
-                bank[:].rearrange("p (b w v) -> p b v w", b=2, w=2),
+                z[:].bitcast(F32).rearrange("p (b v w) -> p b v w", b=blocks, w=2),
+                bank[:].rearrange("p (b w v) -> p b v w", b=blocks, w=2),
             )
             return z
 
-        def project(u, z):
-            zq = quantize(f"z{u}", z, HALF, "z0" if u == 1 else "")
-            bank = new_bank()
-            mm(bank[:, 0:HALF], w2q, slice(0, N), zq[0][:], zq[1][:])
-            res = sb(f"res{u}", [P, HALF], F32)
-            nc.scalar.copy(res[:], bank[:, 0:HALF])
-            nc.sync.dma_start(out[:, u * HALF : (u + 1) * HALF], res[:])
+        def project(u, z, w2_q, reuses=""):
+            z_q = quantize(f"z{u}", z, HALF, reuses)
+            bank = product_bank()
+            multiply(bank[:, 0:HALF], w2_q, 0, z_q)
+            result = sbuf(f"result{u}", [P, HALF], F32)
+            nc.scalar.copy(result[:], bank[:, 0:HALF])
+            nc.sync.dma_start(out[:, u * HALF : (u + 1) * HALF], result[:])
 
-        g_a0 = group_columns("a0", a_raw[0], HALF, on_scalar)
-        make_h(0, 0)
-        make_h(1, 0)
-        make_h(0, 1)
-        make_h(1, 1)
-        ga = group_weight_pair("w3a", w3_raw, 0, on_vector)
-        aq[0] = quantize("a0", g_a0, HALF)
-        gb = group_weight_pair("w3b", w3_raw, 1, on_vector)
-        w3q[0] = quantize("w3a", ga, 2 * P)
-        w3q[1] = quantize("w3b", gb, 2 * P)
+        words_0 = pick_words(0)
+        x_q[0] = (words_0, pick_scales(0))
+        words_1 = pick_words(1)
+        w1_grouped = [group_weight_pair(f"w1_{pair}", w1_raw, pair, on_scalar) for pair in range(2)]
+        w1_q[0] = quantize("w1_0", w1_grouped[0], 2 * P)
+        x_q[1] = (words_1, pick_scales(1, reuses="w1_0_grouped"))
+        w1_q[1] = quantize("w1_1", w1_grouped[1], 2 * P)
+        a0_grouped = group_columns("a0", a_raw[0], HALF, on_scalar)
+        for b in range(2):
+            for t in range(2):
+                make_h(t, b)
+
+        w3_grouped = [group_weight_pair("w3_0", w3_raw, 0, on_vector)]
+        a_q[0] = quantize("a0", a0_grouped, HALF)
+        w3_grouped.append(group_weight_pair("w3_1", w3_raw, 1, on_vector))
+        for pair in range(2):
+            w3_q[pair] = quantize(f"w3_{pair}", w3_grouped[pair], 2 * P)
         make_h(2, 0)
-        filters(0, 0)
-        aq[1] = quantize("a1", group_columns("a1", a_raw[1], HALF, on_vector), HALF)
+        make_f(0, 0)
+        for c in (1, 2):
+            a_q[c] = quantize(f"a{c}", group_columns(f"a{c}", a_raw[c], HALF, on_vector), HALF)
         make_h(2, 1)
-        filters(1, 0)
-        filters(0, 1)
+        make_f(1, 0)
+        make_f(0, 1)
         make_h(3, 0)
         make_h(3, 1)
-        messages(0, 0)
-        messages(1, 0)
-        messages(0, 1)
-        aq[2] = quantize("a2", group_columns("a2", a_raw[2], HALF, on_scalar, "f0_0"), HALF)
-        filters(1, 1)
-        messages(1, 1)
-        aq[3] = quantize("a3", group_columns("a3", a_raw[3], HALF, on_scalar, "f1_0"), HALF)
-        filters(2, 0)
-        filters(2, 1)
-        gw = group_columns("w2", w2_raw, N, on_scalar)
-        filters(3, 0)
-        filters(3, 1)
-        z0 = sum_on_tensor(0)
-        messages(2, 0)
-        messages(2, 1)
-        w2q = quantize("w2", gw, N)
-        project(0, z0)
-        messages(3, 0)
-        messages(3, 1)
-        project(1, sum_on_vector(1))
+
+        gather_times_f(0, 0)
+        gather_times_f(1, 0)
+        gather_times_f(0, 1)
+        make_f(1, 1)
+        gather_times_f(1, 1)
+        a_q[3] = quantize("a3", group_columns("a3", a_raw[3], HALF, on_scalar, reuses="f0_0"), HALF)
+        make_f(2, 0)
+        make_f(2, 1)
+        w2_grouped = group_columns("w2", w2_raw, N, on_scalar)
+        make_f(3, 0)
+        make_f(3, 1)
+        z_first = sum_on_tensor(0)
+
+        gather_times_f(2, 0)
+        gather_times_f(2, 1)
+        w2_q = quantize("w2", w2_grouped, N)
+        project(0, z_first, w2_q)
+        gather_times_f(3, 0)
+        gather_times_f(3, 1)
+        project(1, sum_on_vector(1), w2_q, reuses="z0")

from contextlib import ExitStack

import concourse.mybir as mybir
from concourse.masks import make_identity

K, T, S, V, H, N, J = 512, 2048, 1024, 512, 512, 128, 512
FLOPS = 2 * (K * H * S + J * H * S + H * N * V)

F32 = mybir.dt.float32
BF16 = mybir.dt.bfloat16
I32 = mybir.dt.int32
U32 = mybir.dt.uint32
U16 = mybir.dt.uint16
U8 = mybir.dt.uint8
FP8X4 = mybir.dt.float8_e4m3fn_x4
MULT = mybir.AluOpType.mult
ADD = mybir.AluOpType.add
SILU = mybir.ActivationFunctionType.Silu

P = 128
PACK = 4
LINE = 4
GROUP = 16
BANK = 512
HALF = V // 2
PRODUCT_BANKS = 5
TURN_BANKS = 3

CHUNKS = [(d, u) for u in range(2) for d in range(2)]


def tile_picked_dime_none_p_kernel(
    tc, x_words, x_scales, aT, w1, w3, w2, offs, pos1, pos2, out
):
    nc = tc.nc
    with ExitStack() as ctx:
        keep = ctx.enter_context(tc.tile_pool(name="keep", bufs=1))
        psum = ctx.enter_context(tc.psum_pool(name="psum", bufs=1))

        def sbuf(name, shape, dtype, reuses=""):
            return keep.tile(shape, dtype, name=name, tag=reuses or name, align_bytes=64)

        offs_sb = sbuf("offs_sb", [P, S // GROUP], U16)
        pos_sb = [sbuf("pos1_sb", [P, V // GROUP], U16), sbuf("pos2_sb", [P, V // GROUP], U16)]
        scale_table = sbuf("scale_table", [P, T], U8)
        word_table = sbuf("word_table", [P, T], I32)
        w1_raw = sbuf("w1_raw", [P, PACK, H], F32)
        w3_raw = sbuf("w3_raw", [P, PACK, H], F32)
        w2_raw = sbuf("w2_raw", [P, PACK, N], F32)
        a_raw = [sbuf(f"a_raw{c}", [P, PACK, HALF], F32) for c in range(len(CHUNKS))]

        nc.vector.memset(scale_table[:].bitcast(I32), 0)

        warm_in = sbuf("warm_in", [P, 1], F32)
        warm_out = sbuf("warm_out", [P, 1], F32)
        nc.vector.memset(warm_in[:], 0.0)
        nc.scalar.activation(warm_out[:], warm_in[:], SILU)

        identity = sbuf("identity", [P, P], F32)
        make_identity(nc, identity[:])

        a_rows = aT.rearrange("(p j) c -> p j c", j=PACK)

        def load_chunk(c):
            d, u = CHUNKS[c]
            first = d * V + u * HALF
            nc.sync.dma_start(a_raw[c][:], a_rows[:, :, first : first + HALF])

        nc.sync.dma_start(offs_sb[:], offs)
        nc.sync.dma_start(word_table[:], x_words[0].rearrange("p n j -> p (n j)").bitcast(I32))
        nc.sync.dma_start(pos_sb[0][:], pos1)
        nc.sync.dma_start(pos_sb[1][:], pos2)
        for q in range(4):
            nc.sync.dma_start(
                scale_table[32 * q : 32 * q + 4, :].bitcast(I32),
                x_scales[0, 4 * q : 4 * q + 4, :].bitcast(I32),
            )
        nc.sync.dma_start(w1_raw[:], w1.rearrange("(p j) c -> p j c", j=PACK))
        load_chunk(0)
        nc.sync.dma_start(w3_raw[:], w3.rearrange("(p j) c -> p j c", j=PACK))
        for c in range(1, len(CHUNKS)):
            load_chunk(c)
        nc.sync.dma_start(w2_raw[:], w2.rearrange("(p j) c -> p j c", j=PACK))

        on_vector = nc.vector.tensor_copy
        on_scalar = nc.scalar.copy

        def by_lines(rows):
            return rows.rearrange("p j (c i) -> p c j i", i=LINE)

        def side_by_side(grouped):
            return grouped.rearrange("p (c i j) -> p c j i", i=LINE, j=PACK)

        def group_columns(name, raw, width, copy, reuses=""):
            grouped = sbuf(name + "_grouped", [P, width * PACK], BF16, reuses)
            copy(side_by_side(grouped[:]), by_lines(raw[:]))
            return grouped

        def group_weight_pair(name, raw, pair, copy):
            grouped = sbuf(name + "_grouped", [P, 2 * P * PACK], BF16)
            copy(
                grouped[:].rearrange("p (e m j) -> p m j e", e=2, j=PACK),
                raw[:].rearrange("p j (m t) -> p m j t", t=PACK)[:, :, :, 2 * pair : 2 * pair + 2],
            )
            return grouped

        def quantize(name, grouped, width, reuses=""):
            words = sbuf(name + "_words", [P, width], U32, reuses)
            scales = sbuf(name + "_scales", [P, width], U8)
            nc.vector.quantize_mx(out=words[:].bitcast(FP8X4), scales=scales[:], in_=grouped[:])
            return words, scales

        def multiply(result, stationary, first, moving):
            nc.tensor.matmul_mx(
                out=result,
                lhsT=stationary[0][:, first : first + P].bitcast(FP8X4),
                lhsT_scale=stationary[1][:, first : first + P],
                rhs=moving[0][:].bitcast(FP8X4),
                rhs_scale=moving[1][:],
                start=True,
                stop=True,
            )

        def product_bank():
            return psum.tile([P, BANK], F32, name="product_bank", bufs=PRODUCT_BANKS)

        def turn_bank():
            return psum.tile([P, BANK], F32, name="turn_bank", bufs=TURN_BANKS)

        def picked_entries(b):
            return offs_sb[:, b * BANK // GROUP : (b + 1) * BANK // GROUP]

        def pick_words(b):
            picked = sbuf(f"x_words{b}", [P, BANK], U32)
            nc.vector.tensor_copy(picked[:], word_table[:].bitcast(U32).indirect(picked_entries(b)))
            return picked

        def pick_scales(b, reuses=""):
            picked = sbuf(f"x_scales{b}", [P, BANK], U8, reuses)
            nc.vector.tensor_copy(picked[:], scale_table[:].indirect(picked_entries(b)))
            return picked

        h = [sbuf(f"h{t}", [P, S], F32) for t in range(PACK)]
        products = [sbuf(f"products{c}", [P, PACK, HALF], F32) for c in range(len(CHUNKS))]
        w1_q, w3_q, a_q, x_q, f = {}, {}, {}, {}, {}

        def make_h(t, b):
            bank = product_bank()
            multiply(bank[:], w1_q[t // 2], (t % 2) * P, x_q[b])
            nc.scalar.activation(h[t][:, b * BANK : (b + 1) * BANK], bank[:], SILU)

        def make_f(c, pair):
            bank = product_bank()
            for e in range(2):
                multiply(bank[:, e * HALF : (e + 1) * HALF], w3_q[pair], e * P, a_q[c])
            f[c, pair] = sbuf(f"f{c}_{pair}", [P, BANK], F32)
            nc.scalar.copy(f[c, pair][:], bank[:])

        def gather_times_f(c, pair):
            d, u = CHUNKS[c]
            places = pos_sb[d][:, u * HALF // GROUP : (u + 1) * HALF // GROUP]
            for e in range(2):
                t = 2 * pair + e
                nc.vector.tensor_tensor(
                    products[c][:, t, :],
                    h[t][:].indirect(places),
                    f[c, pair][:, e * HALF : (e + 1) * HALF],
                    MULT,
                )

        def sum_on_vector(u):
            z = sbuf(f"z{u}", [P, HALF * PACK], BF16)
            nc.vector.tensor_tensor(
                side_by_side(z[:]), by_lines(products[2 * u][:]), by_lines(products[2 * u + 1][:]), ADD
            )
            return z

        def sum_on_tensor(u):
            blocks = HALF // P
            turned = []
            for block in range(blocks):
                bank = turn_bank()
                for t in range(PACK):
                    for d in range(2):
                        nc.tensor.matmul(
                            bank[:, t * P : (t + 1) * P],
                            lhsT=products[2 * u + d][:, t, block * P : (block + 1) * P],
                            rhs=identity[:],
                            is_transpose=True,
                            start=(d == 0),
                            stop=(d == 1),
                        )
                z_turned = sbuf(f"z_turned{block}", [P, H], BF16)
                nc.scalar.copy(
                    z_turned[:].rearrange("v (w m e) -> v w m e", w=2, e=2),
                    bank[:].rearrange("v (w e m) -> v w m e", w=2, e=2),
                )
                turned.append(z_turned)
            bank = turn_bank()
            for block in range(blocks):
                pairs = turned[block][:].bitcast(F32)
                for w in range(2):
                    first = (2 * block + w) * P
                    nc.tensor.transpose(
                        bank[:, first : first + P], pairs[:, w * P : (w + 1) * P], identity[:]
                    )
            z = sbuf(f"z{u}", [P, HALF * PACK], BF16)
            nc.scalar.copy(
                z[:].bitcast(F32).rearrange("p (b v w) -> p b v w", b=blocks, w=2),
                bank[:].rearrange("p (b w v) -> p b v w", b=blocks, w=2),
            )
            return z

        def project(u, z, w2_q, reuses=""):
            z_q = quantize(f"z{u}", z, HALF, reuses)
            bank = product_bank()
            multiply(bank[:, 0:HALF], w2_q, 0, z_q)
            result = sbuf(f"result{u}", [P, HALF], F32)
            nc.scalar.copy(result[:], bank[:, 0:HALF])
            nc.sync.dma_start(out[:, u * HALF : (u + 1) * HALF], result[:])

        words_0 = pick_words(0)
        x_q[0] = (words_0, pick_scales(0))
        words_1 = pick_words(1)
        w1_grouped = [group_weight_pair(f"w1_{pair}", w1_raw, pair, on_scalar) for pair in range(2)]
        w1_q[0] = quantize("w1_0", w1_grouped[0], 2 * P)
        x_q[1] = (words_1, pick_scales(1, reuses="w1_0_grouped"))
        w1_q[1] = quantize("w1_1", w1_grouped[1], 2 * P)
        a0_grouped = group_columns("a0", a_raw[0], HALF, on_scalar)
        for b in range(2):
            for t in range(2):
                make_h(t, b)

        w3_grouped = [group_weight_pair("w3_0", w3_raw, 0, on_vector)]
        a_q[0] = quantize("a0", a0_grouped, HALF)
        w3_grouped.append(group_weight_pair("w3_1", w3_raw, 1, on_vector))
        for pair in range(2):
            w3_q[pair] = quantize(f"w3_{pair}", w3_grouped[pair], 2 * P)
        make_h(2, 0)
        make_f(0, 0)
        for c in (1, 2):
            a_q[c] = quantize(f"a{c}", group_columns(f"a{c}", a_raw[c], HALF, on_vector), HALF)
        make_h(2, 1)
        make_f(1, 0)
        make_f(0, 1)
        make_h(3, 0)
        make_h(3, 1)

        gather_times_f(0, 0)
        gather_times_f(1, 0)
        gather_times_f(0, 1)
        make_f(1, 1)
        gather_times_f(1, 1)
        a_q[3] = quantize("a3", group_columns("a3", a_raw[3], HALF, on_scalar, reuses="f0_0"), HALF)
        make_f(2, 0)
        make_f(2, 1)
        w2_grouped = group_columns("w2", w2_raw, N, on_scalar)
        make_f(3, 0)
        make_f(3, 1)
        z_first = sum_on_tensor(0)

        gather_times_f(2, 0)
        gather_times_f(2, 1)
        w2_q = quantize("w2", w2_grouped, N)
        project(0, z_first, w2_q)
        gather_times_f(3, 0)
        gather_times_f(3, 1)
        project(1, sum_on_vector(1), w2_q, reuses="z0")
